import numpy as np
import ml_dtypes


def mxq(x, axis, fmt="e4m3"):
    dtype, down = {"e4m3": (ml_dtypes.float8_e4m3fn, 7), "e5m2": (ml_dtypes.float8_e5m2, 14)}[fmt]
    v = np.moveaxis(np.asarray(x, np.float32).astype(ml_dtypes.bfloat16).astype(np.float64), axis, -1)
    blocks = v.reshape(v.shape[:-1] + (-1, 32))
    amax = np.abs(blocks).max(-1, keepdims=True)
    byte = np.maximum(np.where(amax > 0, np.frexp(amax)[1] - 1 + 127, 0) - down, 1)
    scale = np.exp2(byte - 127.0)
    codes = (blocks / scale).astype(np.float32).astype(dtype).astype(np.float64)
    return np.moveaxis((codes * scale).reshape(v.shape), -1, axis)


WIDE = False


def mx_kscale(k):
    if not WIDE:
        return np.ones(k)
    levels = np.array([10, -10, 5, -5, 0])
    if k % 512:
        return np.exp2(np.random.permutation(np.resize(levels, k // 32))).repeat(32)
    a = np.empty((k // 512, 16))
    for p in range(k // 512):
        a[p, :8] = np.random.permutation(np.resize(levels, 8))
        for g in range(8):
            far = levels[np.abs(levels - a[p, g]) >= 10]
            a[p, g + 8] = far[np.random.randint(len(far))]
    return np.exp2(a.ravel()).repeat(32)


def f64(x):
    return np.asarray(x).astype(np.float64)


def striped(idx):
    return np.tile(idx.reshape(-1, 16).T, (8, 1)).astype(np.uint16)


def unstriped(offs):
    return offs[:16].T.reshape(-1).astype(np.int64)


E2M1 = np.array([0.0, 0.5, 1.0, 1.5, 2.0, 3.0, 4.0, 6.0, -0.0, -0.5, -1.0, -1.5, -2.0, -3.0, -4.0, -6.0])


def pack_weight(w, fmt):
    k, n = w.shape
    w = f64(np.asarray(w, np.float32).astype(ml_dtypes.bfloat16)).reshape(k // 32, 32, n)
    amax = np.abs(w).max(1)
    if fmt == "e4m3":
        byte = np.frexp(amax)[1] - 1 + 127 - 7
    else:
        mant, ex = np.frexp(amax / 6.0)
        byte = np.where(mant > 0.5, ex, ex - 1) + 127
    byte = np.clip(np.where(amax > 0, byte, 1), 1, 254)
    scaled = (w * np.exp2(127.0 - byte)[:, None, :]).reshape(k, n).astype(np.float32)
    by_word = np.ascontiguousarray(scaled.reshape(k // 512, 128, 4, n).transpose(0, 1, 3, 2))
    if fmt == "e4m3":
        words = by_word.astype(ml_dtypes.float8_e4m3fn).view(np.uint8)
    else:
        c = by_word.astype(ml_dtypes.float4_e2m1fn).view(np.uint8) & 0xF
        words = (c[..., 0::2] | (c[..., 1::2] << 4)).reshape(k // 512, 128, 2 * n)
    return np.ascontiguousarray(words), np.ascontiguousarray(byte.astype(np.uint8).reshape(k // 512, 16, n))


def unpack_weight(words, scales, fmt):
    g, _, n = scales.shape
    words = np.ascontiguousarray(words).reshape(g, 128, n, -1)
    if fmt == "e4m3":
        vals = words.view(ml_dtypes.float8_e4m3fn).astype(np.float64)
    else:
        nib = np.empty((g, 128, n, 4), np.uint8)
        nib[..., 0::2] = words & 0xF
        nib[..., 1::2] = words >> 4
        vals = E2M1[nib]
    vals = vals * np.repeat(np.exp2(scales.astype(np.float64) - 127.0), 8, axis=1)[..., None]
    return vals.transpose(0, 1, 3, 2).reshape(g * 512, n)


def gelu(v):
    return 0.5 * v * (1.0 + np.tanh(np.sqrt(2.0 / np.pi) * (v + 0.044715 * v**3)))


def striped8(idx):
    return np.concatenate([v.reshape(-1, 16).T for v in idx]).astype(np.uint16)


def unstriped8(offs):
    return np.stack([offs[16 * g:16 * g + 16].T.reshape(-1) for g in range(8)]).astype(np.int64)


def heads(h, wgt, idx8):
    r = np.arange(h.shape[0])
    return wgt[r // 4 % 128] * h[r[:, None], idx8[r % 512 // 64]]


def put_heads(h, wgs, idx8, t2):
    r = np.arange(h.shape[0])
    page = np.zeros((h.shape[0], t2))
    page[r[:, None], idx8[r % 512 // 64]] = wgs[r // 4 % 128] * h
    return page


K, T, S, H, P, N, T2 = 1536, 4096, 1024, 1024, 512, 512, 1024

def setup_inputs():
    n = np.random.standard_normal
    s = mx_kscale(K)[:, None]
    u = mx_kscale(H)[:, None]
    d = {}
    d["tab_words"], d["tab_scales"] = pack_weight(n((K, T)) * s, "e4m3")
    d["offs"] = striped(np.random.permutation(T)[:S])
    d["w1"] = (n((K, H)) / K ** 0.5 / s * u.T).astype(np.float32)
    d["b1"] = (0.6 * n(H) * u[:, 0]).astype(np.float32)
    d["offs2"] = striped8(np.stack([np.random.permutation(S)[:P] for _ in range(8)]))
    d["wgt"] = np.repeat(np.random.uniform(0.5, 2.0, (8, P)), 16, axis=0).astype(np.float32)
    d["view"] = np.exp(0.5 * n((H, P))).astype(np.float32)
    d["w4_words"], d["w4_scales"] = pack_weight(0.6 * n((H, N)) / H ** 0.5 / u, "e2m1")
    d["w5"] = (0.6 * n((H, N)) / H ** 0.5 / u).astype(np.float32)
    d["shift"] = (0.7 * n((N, P))).astype(np.float32)
    d["offs3"] = striped8(np.stack([np.random.permutation(T2)[:P] for _ in range(8)]))
    d["wgo"] = np.repeat(np.random.uniform(0.5, 2.0, (8, P)), 16, axis=0).astype(np.float32)
    return d

def reference(tab_words, tab_scales, offs, w1, b1, offs2, wgt, view,
              w4_words, w4_scales, w5, shift, offs3, wgo):
    v = unpack_weight(tab_words, tab_scales, "e4m3")[:, unstriped(offs)]
    h = (mxq(f64(w1), 0, "e4m3").T @ v) + f64(b1)[:, None]
    x = heads(h, f64(wgt), unstriped8(offs2))
    z = mxq(x * f64(view), 0, "e4m3")
    e4 = unpack_weight(w4_words, w4_scales, "e2m1").T @ z
    e5 = mxq(f64(w5), 0, "e4m3").T @ z
    y = np.maximum(e4, e5) + f64(shift)
    return put_heads(y, f64(wgo), unstriped8(offs3), T2)

@@ -1,0 +1,379 @@
+from contextlib import ExitStack
+
+import concourse.mybir as mybir
+from concourse.masks import make_identity
+
+K, T, S, H, M, N, T2 = 1536, 4096, 1024, 1024, 512, 512, 1024
+FLOPS = 2 * K * H * S + 2 * 2 * H * N * M
+
+F32 = mybir.dt.float32
+BF16 = mybir.dt.bfloat16
+I32 = mybir.dt.int32
+U32 = mybir.dt.uint32
+U16 = mybir.dt.uint16
+U8 = mybir.dt.uint8
+FP8X4 = mybir.dt.float8_e4m3fn_x4
+FP4X4 = mybir.dt.float4_e2m1fn_x4
+MULT = mybir.AluOpType.mult
+MAX = mybir.AluOpType.max
+IDENTITY = mybir.ActivationFunctionType.Identity
+
+P = 128
+PACK = 4
+PASS = P * PACK
+BANK = 512
+HALF = 256
+
+
+def tile_list_dome_patch_corrections_kernel(
+    tc, tab_words, tab_scales, offs, w1, b1, offs2, wgt, view,
+    w4_words, w4_scales, w5, shift, offs3, wgo, out,
+):
+    nc = tc.nc
+    with ExitStack() as ctx:
+        lists = ctx.enter_context(tc.tile_pool(name="lists", bufs=1))
+        keep = ctx.enter_context(tc.tile_pool(name="keep", bufs=1))
+        ring = ctx.enter_context(tc.tile_pool(name="ring", bufs=1))
+        arena = ctx.enter_context(tc.tile_pool(name="arena", bufs=1))
+        psum = ctx.enter_context(tc.psum_pool(name="psum", bufs=8))
+
+        def bank(name):
+            return psum.tile([P, BANK], F32, name=name, tag="bank")
+
+        def placed(shape, dtype, name, kib):
+            return arena.tile(shape, dtype, name=name, align_bytes=64, offset=1024 * kib)
+
+        def round_copy(engine, dst, src):
+            if engine == "vector":
+                nc.vector.tensor_copy(out=dst, in_=src)
+            else:
+                nc.scalar.copy(out=dst, in_=src)
+
+        def deal_round(engine, grouped, raw, m0):
+            width = raw.shape[2] // PACK
+            dst = grouped.rearrange("p (t m j) -> p m j t", t=PACK, j=PACK)[:, m0 : m0 + width, :, :]
+            round_copy(engine, dst, raw[:].rearrange("p j (m t) -> p m j t", t=PACK))
+
+        def quantise(codes, scales, grouped):
+            nc.vector.quantize_mx(out=codes.bitcast(FP8X4), scales=scales, in_=grouped)
+
+        tab_scale = keep.tile([P, T], U8, name="tab_scale", align_bytes=64)
+        nc.vector.memset(tab_scale[:].bitcast(I32), 0)
+        w4_scale = keep.tile([P, 2, N], U8, name="w4_scale", align_bytes=64)
+        nc.vector.memset(w4_scale[:].bitcast(I32), 0)
+        pages = [keep.tile([P, T2], F32, name="page%d" % i) for i in range(PACK)]
+        for page in pages:
+            nc.vector.memset(page[:], 0.0)
+
+        bias = keep.tile([P, 2, PACK], F32, name="bias")
+        ident = keep.tile([P, P], F32, name="ident")
+        make_identity(nc, ident[:])
+
+        idx = lists.tile([P, S // 16], U16, name="idx")
+        idx2 = lists.tile([P, M // 16], U16, name="idx2")
+        idx3 = lists.tile([P, M // 16], U16, name="idx3")
+
+        def load_table(a):
+            words = placed([P, T], U32, "tab%d" % a, 16 * a)
+            nc.sync.dma_start(
+                out=words[:].bitcast(I32),
+                in_=tab_words[a].rearrange("p t i -> p (t i)").bitcast(I32),
+            )
+            return words
+
+        def rows4(matrix, r0, c0, width):
+            return matrix[r0 : r0 + PASS, c0 : c0 + width].rearrange("(p j) c -> p j c", j=PACK)
+
+        def load_w1(a, b, kib):
+            raw = placed([P, PACK, PASS], F32, "w1raw%d%d" % (a, b), kib)
+            nc.sync.dma_start(out=raw[:], in_=rows4(w1, PASS * a, PASS * b, PASS))
+            return raw
+
+        def load_view(b):
+            tiles = []
+            for u in range(2):
+                factor = keep.tile([P, 2, M], F32, name="view%d%d" % (b, u))
+                nc.sync.dma_start(out=factor[:], in_=rows4(view, PASS * b, 0, M)[:, 2 * u : 2 * u + 2, :])
+                tiles.append(factor)
+            return tiles
+
+        nc.sync.dma_start(idx[:], offs)
+        tab = [load_table(0)]
+        for q in range(4):
+            nc.sync.dma_start(
+                out=tab_scale[32 * q : 32 * q + 12, :].bitcast(I32),
+                in_=tab_scales[:, 4 * q : 4 * q + 4, :].bitcast(I32),
+            )
+        w1_raw = {(0, 0): load_w1(0, 0, 48)}
+        nc.sync.dma_start(idx2[:], offs2)
+        nc.sync.dma_start(out=bias[:], in_=b1.rearrange("(b p i) -> p b i", b=2, i=PACK))
+        tab.append(load_table(1))
+        w1_raw[(1, 0)] = load_w1(1, 0, 56)
+        tab.append(load_table(2))
+        last_raw = []
+        for u in range(2):
+            raw = keep.tile([P, PACK, HALF], F32, name="w1last%d" % u)
+            nc.sync.dma_start(out=raw[:], in_=rows4(w1, PASS * 2, HALF * u, HALF))
+            last_raw.append(raw)
+        wgt_sb = keep.tile([P, M], F32, name="wgt_sb")
+        nc.sync.dma_start(out=wgt_sb[:], in_=wgt)
+        view0 = load_view(0)
+        w1_raw[(0, 1)] = load_w1(0, 1, 64)
+
+        v_codes = []
+        v_scale = keep.tile([P, S], U8, name="v_scale", align_bytes=64)
+        for a in range(3):
+            picked = keep.tile([P, S], U32, name="v_codes%d" % a, align_bytes=64)
+            nc.vector.tensor_copy(out=picked[:], in_=tab[a][:].indirect(idx[:]))
+            v_codes.append(picked)
+            if a == 0:
+                nc.vector.tensor_copy(out=v_scale[:], in_=tab_scale[:].indirect(idx[:]))
+
+        def grouped_tile(name):
+            return ring.tile([P, PASS * PACK], BF16, name=name, tag="grouped", bufs=3, align_bytes=64)
+
+        def w1_planes(a, b):
+            codes = ring.tile([P, PASS], U32, name="w1c%d%d" % (a, b), tag="w1c", bufs=4, align_bytes=64)
+            scales = ring.tile([P, PASS], U8, name="w1s%d%d" % (a, b), tag="w1s", bufs=4, align_bytes=64)
+            return codes, scales
+
+        def first_pass(acc, planes, a, i, start, stop):
+            codes, scales = planes
+            cols = slice(P * i, P * (i + 1))
+            for u in range(2):
+                entries = slice(BANK * u, BANK * (u + 1))
+                nc.tensor.matmul_mx(
+                    out=acc[i][u][:],
+                    lhsT=codes[:, cols].bitcast(FP8X4),
+                    lhsT_scale=scales[:, cols],
+                    rhs=v_codes[a][:, entries].bitcast(FP8X4),
+                    rhs_scale=v_scale[4 * a : P, entries],
+                    start=start,
+                    stop=stop,
+                )
+
+        def empty_h(acc, b, i):
+            h = ring.tile([P, S], F32, name="h%d%d" % (b, i), tag="h", bufs=8)
+            for u in range(2):
+                nc.scalar.activation(
+                    out=h[:, BANK * u : BANK * (u + 1)], in_=acc[i][u][:], func=IDENTITY,
+                    bias=bias[:, b, i : i + 1],
+                )
+            return h
+
+        def interleave(grouped, picked):
+            nc.scalar.copy(
+                out=grouped.rearrange("p (c e i) -> p c i e", e=4, i=PACK),
+                in_=picked.rearrange("p i (c e) -> p c i e", e=4),
+            )
+
+        acc0 = [[bank("h0_%d%d" % (i, u)) for u in range(2)] for i in range(PACK)]
+        for a in range(2):
+            grouped = grouped_tile("g%d0" % a)
+            deal_round("scalar", grouped[:], w1_raw[(a, 0)], 0)
+            planes = w1_planes(a, 0)
+            quantise(planes[0][:], planes[1][:], grouped[:])
+            for i in range(PACK):
+                first_pass(acc0, planes, a, i, a == 0, False)
+        w1_raw[(1, 1)] = load_w1(1, 1, 0)
+        w1_raw[(2, 1)] = load_w1(2, 1, 8)
+
+        def load_w5(a):
+            raw = placed([P, PACK, N], F32, "w5raw%d" % a, 16 + 16 * a)
+            nc.sync.dma_start(out=raw[:], in_=rows4(w5, PASS * a, 0, N))
+            return raw
+
+        w5_raw = [load_w5(0)]
+        view1 = placed([P, PACK, M], F32, "view1", 24)
+        nc.sync.dma_start(out=view1[:], in_=rows4(view, PASS, 0, M))
+        w5_raw.append(load_w5(1))
+        shift_sb = placed([P, PACK, M], F32, "shift_sb", 40)
+        nc.sync.dma_start(out=shift_sb[:], in_=rows4(shift, 0, 0, M))
+        w4_codes = keep.tile([P, 2, 2 * N], U8, name="w4_codes", align_bytes=64)
+        nc.sync.dma_start(
+            out=w4_codes[:].bitcast(I32), in_=w4_words.rearrange("a p c -> p a c").bitcast(I32)
+        )
+        for q in range(4):
+            nc.sync.dma_start(
+                out=w4_scale[32 * q : 32 * q + 4, :, :].bitcast(I32),
+                in_=w4_scales[:, 4 * q : 4 * q + 4, :].rearrange("a r c -> r a c").bitcast(I32),
+            )
+        wgo_sb = keep.tile([P, M], F32, name="wgo_sb")
+        nc.sync.dma_start(out=wgo_sb[:], in_=wgo)
+        nc.sync.dma_start(idx3[:], offs3)
+
+        grouped = grouped_tile("g20")
+        deal_round("scalar", grouped[:], last_raw[0], 0)
+        deal_round("vector", grouped[:], last_raw[1], HALF // PACK)
+        planes = w1_planes(2, 0)
+        for i in range(PACK):
+            cols = slice(P * i, P * (i + 1))
+            quantise(planes[0][:, cols], planes[1][:, cols], grouped[:, PASS * i : PASS * (i + 1)])
+            first_pass(acc0, planes, 2, i, False, True)
+
+        x0_bytes = keep.tile([P, (PACK + 1) * M], F32, name="x0", align_bytes=64)
+        x0 = x0_bytes[:, 0 : PACK * M].rearrange("p (i m) -> p i m", i=PACK)
+
+        def pick0(i):
+            h = empty_h(acc0, 0, i)
+            row = view0[i // 2][:, i % 2, :]
+            nc.vector.tensor_tensor(out=row, in0=row, in1=wgt_sb[:], op=MULT)
+            return h, row
+
+        def gather0(i, h, row):
+            nc.vector.tensor_tensor(
+                out=x0_bytes[:, M * i : M * (i + 1)], in0=h[:].indirect(idx2[:]), in1=row, op=MULT
+            )
+
+        acc1 = [[bank("h1_%d%d" % (i, u)) for u in range(2)] for i in range(PACK)]
+
+        def w1_second(a, engine, grouped):
+            deal_round(engine, grouped, w1_raw[(a, 1)], 0)
+            planes = w1_planes(a, 1)
+            quantise(planes[0][:], planes[1][:], grouped)
+            return planes
+
+        gather0(0, *pick0(0))
+        gather0(1, *pick0(1))
+        planes = w1_second(0, "scalar", grouped_tile("g01")[:])
+        gather0(2, *pick0(2))
+        held = pick0(3)
+        for i in range(PACK):
+            first_pass(acc1, planes, 0, i, True, False)
+        planes2 = w1_second(2, "vector", grouped_tile("g21")[:])
+        planes1 = w1_second(1, "scalar", x0_bytes[:, (PACK - 1) * M : (PACK + 1) * M].bitcast(BF16))
+        gather0(3, *held)
+
+        w5_planes = []
+
+        def w5_operand(a, engine):
+            grouped = grouped_tile("g5%d" % a)
+            deal_round(engine, grouped[:], w5_raw[a], 0)
+            codes = keep.tile([P, N], U32, name="w5c%d" % a, align_bytes=64)
+            scales = keep.tile([P, N], U8, name="w5s%d" % a, align_bytes=64)
+            quantise(codes[:], scales[:], grouped[:])
+            w5_planes.append((codes, scales))
+
+        h1 = []
+        for i in range(PACK):
+            first_pass(acc1, planes2, 2, i, False, False)
+            first_pass(acc1, planes1, 1, i, False, True)
+            h1.append(empty_h(acc1, 1, i))
+        w5_operand(0, "scalar")
+
+        pieces = ((0, P), (P, P), (2 * P, 2 * P))
+        rest = M - P
+        weights = keep.tile([P, PACK * rest], F32, name="weights")
+
+        def weigh1(m0, width):
+            factor = weights[:, 0 : PACK * width].rearrange("p (i m) -> p i m", i=PACK)
+            nc.vector.tensor_tensor(
+                out=factor,
+                in0=view1[:, :, m0 : m0 + width],
+                in1=wgt_sb[:, m0 : m0 + width].unsqueeze(1).to_broadcast([P, PACK, width]),
+                op=MULT,
+            )
+            return factor
+
+        def gather1(s, factor, f0):
+            m0, width = pieces[s]
+            x1 = placed([P, PACK, width], F32, "x1_%d" % s, 48 + m0 // 64)
+            for i in range(PACK):
+                nc.vector.tensor_tensor(
+                    out=x1[:, i, :],
+                    in0=h1[i][:].indirect(idx2[:, m0 // 16 : (m0 + width) // 16]),
+                    in1=factor[:, i, m0 - f0 : m0 - f0 + width],
+                    op=MULT,
+                )
+            return x1
+
+        def z_operand(s, x1):
+            m0, width = pieces[s]
+            grouped = placed([P, 2 * PACK * width], BF16, "gz%d" % s, 64 + m0 // 64)
+            interleave(grouped[:, PACK * width : 2 * PACK * width], x1[:])
+            interleave(grouped[:, 0 : PACK * width], x0[:, :, m0 : m0 + width])
+            codes = keep.tile([P, 2 * width], U32, name="z_codes%d" % s, align_bytes=64)
+            scales = keep.tile([P, 2 * width], U8, name="z_scale%d" % s, align_bytes=64)
+            quantise(codes[:], scales[:], grouped[:])
+            return codes, scales, width
+
+        def open_y(c):
+            turned = bank("shift_ps%d" % c)
+            for i in range(PACK):
+                nc.tensor.transpose(turned[:, P * i : P * (i + 1)], shift_sb[:, i, P * c : P * (c + 1)], ident[:])
+            shift_t = ring.tile([P, BANK], F32, name="shift_t%d" % c, tag="shift_t", bufs=2)
+            nc.scalar.copy(out=shift_t[:], in_=turned[:])
+            y_ps = bank("y_ps%d" % c)
+            for i in range(PACK):
+                cols = slice(P * i, P * (i + 1))
+                nc.tensor.matmul(
+                    y_ps[:, cols], shift_t[:, cols], ident[:], start=(i == 0), stop=False, is_transpose=True
+                )
+            return y_ps
+
+        def proposals(c, z, w):
+            codes, scales, width = z
+            e4 = bank("e4_%d" % c)
+            e5 = bank("e5_%d" % c)
+            cols = [slice(width * a + P * w, width * a + P * (w + 1)) for a in range(2)]
+            for a in range(2):
+                nc.tensor.matmul_mx(
+                    out=e4[:], lhsT=codes[:, cols[a]].bitcast(FP8X4), lhsT_scale=scales[:, cols[a]],
+                    rhs=w4_codes[:, a, :].bitcast(FP4X4), rhs_scale=w4_scale[:, a, :],
+                    start=(a == 0), stop=(a == 1),
+                )
+            for a in range(2):
+                nc.tensor.matmul_mx(
+                    out=e5[:], lhsT=codes[:, cols[a]].bitcast(FP8X4), lhsT_scale=scales[:, cols[a]],
+                    rhs=w5_planes[a][0][:].bitcast(FP8X4), rhs_scale=w5_planes[a][1][:],
+                    start=(a == 0), stop=(a == 1),
+                )
+            e4_sb = ring.tile([P, N], F32, name="e4_sb%d" % c, tag="e4_sb", bufs=2)
+            nc.scalar.copy(
+                out=e4_sb[:].rearrange("m (i p) -> m i p", i=PACK),
+                in_=e4[:].rearrange("m (p i) -> m i p", i=PACK),
+            )
+            larger = ring.tile([P, N], F32, name="larger%d" % c, tag="larger", bufs=3)
+            nc.vector.tensor_tensor(out=larger[:], in0=e5[:], in1=e4_sb[:], op=MAX)
+            return larger
+
+        def close_y(y_ps, larger, y, w):
+            for i in range(PACK):
+                cols = slice(P * i, P * (i + 1))
+                nc.tensor.matmul(
+                    y_ps[:, cols], larger[:, cols], ident[:], start=False, stop=(i == PACK - 1), is_transpose=True
+                )
+            nc.scalar.copy(out=y[:, :, P * w : P * (w + 1)], in_=y_ps[:].rearrange("p (i m) -> p i m", i=PACK))
+
+        def place(s, y, store):
+            m0, width = pieces[s]
+            for i in range(PACK):
+                nc.vector.tensor_tensor(
+                    out=pages[i][:].indirect(idx3[:, m0 // 16 : (m0 + width) // 16]),
+                    in0=y[:, i, :],
+                    in1=wgo_sb[:, m0 : m0 + width],
+                    op=MULT,
+                )
+                if store:
+                    nc.sync.dma_start(out=rows4(out, 0, 0, T2)[:, i, :], in_=pages[i][:])
+
+        ys = [placed([P, PACK, width], F32, "y%d" % s, 56 + m0 // 64) for s, (m0, width) in enumerate(pieces)]
+        x1 = gather1(0, weigh1(0, P), 0)
+        w5_operand(1, "vector")
+        z = z_operand(0, x1)
+        y_ps0 = open_y(0)
+        larger0 = proposals(0, z, 0)
+        close_y(y_ps0, larger0, ys[0], 0)
+        factor = weigh1(P, rest)
+        z = z_operand(1, gather1(1, factor, P))
+        y_ps1 = open_y(1)
+        larger1 = proposals(1, z, 0)
+        z = z_operand(2, gather1(2, factor, P))
+        place(0, ys[0], False)
+        larger2 = proposals(2, z, 0)
+        larger3 = proposals(3, z, 1)
+        close_y(y_ps1, larger1, ys[1], 0)
+        close_y(open_y(2), larger2, ys[2], 0)
+        close_y(open_y(3), larger3, ys[2], 1)
+        place(1, ys[1], False)
+        place(2, ys[2], True)

@@ -23,6 +23,7 @@ PACK = 4
 PASS = P * PACK
 BANK = 512
 HALF = 256
+ROW = 384
 
 
 def tile_list_dome_patch_corrections_kernel(
@@ -89,13 +90,10 @@ def tile_list_dome_patch_corrections_kernel(
             nc.sync.dma_start(out=raw[:], in_=rows4(w1, PASS * a, PASS * b, PASS))
             return raw
 
-        def load_view(b):
-            tiles = []
-            for u in range(2):
-                factor = keep.tile([P, 2, M], F32, name="view%d%d" % (b, u))
-                nc.sync.dma_start(out=factor[:], in_=rows4(view, PASS * b, 0, M)[:, 2 * u : 2 * u + 2, :])
-                tiles.append(factor)
-            return tiles
+        def load_view0(u):
+            factor = keep.tile([P, 2, M], F32, name="view0%d" % u)
+            nc.sync.dma_start(out=factor[:], in_=rows4(view, 0, 0, M)[:, 2 * u : 2 * u + 2, :])
+            return factor
 
         nc.sync.dma_start(idx[:], offs)
         tab = [load_table(0)]
@@ -117,8 +115,9 @@ def tile_list_dome_patch_corrections_kernel(
             last_raw.append(raw)
         wgt_sb = keep.tile([P, M], F32, name="wgt_sb")
         nc.sync.dma_start(out=wgt_sb[:], in_=wgt)
-        view0 = load_view(0)
+        view0 = [load_view0(0)]
         w1_raw[(0, 1)] = load_w1(0, 1, 64)
+        view0.append(load_view0(1))
 
         v_codes = []
         v_scale = keep.tile([P, S], U8, name="v_scale", align_bytes=64)
@@ -211,8 +210,8 @@ def tile_list_dome_patch_corrections_kernel(
             quantise(planes[0][:, cols], planes[1][:, cols], grouped[:, PASS * i : PASS * (i + 1)])
             first_pass(acc0, planes, 2, i, False, True)
 
-        x0_bytes = keep.tile([P, (PACK + 1) * M], F32, name="x0", align_bytes=64)
-        x0 = x0_bytes[:, 0 : PACK * M].rearrange("p (i m) -> p i m", i=PACK)
+        x0_bytes = keep.tile([P, PACK * 2 * M], F32, name="x0", align_bytes=64)
+        x0 = x0_bytes[:].rearrange("p (i m) -> p i m", i=PACK)[:, :, 0:M]
 
         def pick0(i):
             h = empty_h(acc0, 0, i)
@@ -222,7 +221,7 @@ def tile_list_dome_patch_corrections_kernel(
 
         def gather0(i, h, row):
             nc.vector.tensor_tensor(
-                out=x0_bytes[:, M * i : M * (i + 1)], in0=h[:].indirect(idx2[:]), in1=row, op=MULT
+                out=x0[:, i, :], in0=h[:].indirect(idx2[:]), in1=row, op=MULT
             )
 
         acc1 = [[bank("h1_%d%d" % (i, u)) for u in range(2)] for i in range(PACK)]
@@ -241,7 +240,7 @@ def tile_list_dome_patch_corrections_kernel(
         for i in range(PACK):
             first_pass(acc1, planes, 0, i, True, False)
         planes2 = w1_second(2, "vector", grouped_tile("g21")[:])
-        planes1 = w1_second(1, "scalar", x0_bytes[:, (PACK - 1) * M : (PACK + 1) * M].bitcast(BF16))
+        planes1 = w1_second(1, "scalar", x0_bytes[:, 6 * M : 8 * M].bitcast(BF16))
         gather0(3, *held)
 
         w5_planes = []
@@ -261,41 +260,41 @@ def tile_list_dome_patch_corrections_kernel(
             h1.append(empty_h(acc1, 1, i))
         w5_operand(0, "scalar")
 
-        pieces = ((0, P), (P, P), (2 * P, 2 * P))
-        rest = M - P
-        weights = keep.tile([P, PACK * rest], F32, name="weights")
+        x1_bytes = placed([P, PACK * ROW], F32, "x1", 48)
+        x1 = (
+            x1_bytes[:, 0 : PACK * HALF].rearrange("p (i m) -> p i m", i=PACK),
+            x1_bytes[:].rearrange("p (i m) -> p i m", i=PACK)[:, :, 0:HALF],
+        )
 
-        def weigh1(m0, width):
-            factor = weights[:, 0 : PACK * width].rearrange("p (i m) -> p i m", i=PACK)
+        def gather1(u, i):
             nc.vector.tensor_tensor(
-                out=factor,
-                in0=view1[:, :, m0 : m0 + width],
-                in1=wgt_sb[:, m0 : m0 + width].unsqueeze(1).to_broadcast([P, PACK, width]),
+                out=x1[u][:, i, :],
+                in0=h1[i][:].indirect(idx2[:, 16 * u : 16 * (u + 1)]),
+                in1=view1[:, i, HALF * u : HALF * (u + 1)],
                 op=MULT,
             )
-            return factor
 
-        def gather1(s, factor, f0):
-            m0, width = pieces[s]
-            x1 = placed([P, PACK, width], F32, "x1_%d" % s, 48 + m0 // 64)
-            for i in range(PACK):
-                nc.vector.tensor_tensor(
-                    out=x1[:, i, :],
-                    in0=h1[i][:].indirect(idx2[:, m0 // 16 : (m0 + width) // 16]),
-                    in1=factor[:, i, m0 - f0 : m0 - f0 + width],
-                    op=MULT,
-                )
-            return x1
-
-        def z_operand(s, x1):
-            m0, width = pieces[s]
-            grouped = placed([P, 2 * PACK * width], BF16, "gz%d" % s, 64 + m0 // 64)
-            interleave(grouped[:, PACK * width : 2 * PACK * width], x1[:])
-            interleave(grouped[:, 0 : PACK * width], x0[:, :, m0 : m0 + width])
-            codes = keep.tile([P, 2 * width], U32, name="z_codes%d" % s, align_bytes=64)
-            scales = keep.tile([P, 2 * width], U8, name="z_scale%d" % s, align_bytes=64)
+        def z_operand(name, grouped):
+            codes = keep.tile([P, HALF], U32, name="%s_codes" % name, align_bytes=64)
+            scales = keep.tile([P, HALF], U8, name="%s_scale" % name, align_bytes=64)
             quantise(codes[:], scales[:], grouped[:])
-            return codes, scales, width
+            return codes, scales
+
+        def z_upper(u):
+            grouped = placed([P, PACK * HALF], BF16, "gz0_%d" % u, 64 + 2 * u)
+            interleave(grouped[:], x0[:, :, HALF * u : HALF * (u + 1)])
+            return z_operand("z0_%d" % u, grouped)
+
+        def z_lower_rows(u):
+            grouped = placed([P, PACK * HALF], BF16, "gz1_%d" % u, 68 + 2 * u)
+            weight = wgt_sb[:, HALF * u : HALF * (u + 1)].rearrange("p (c e) -> p c e", e=2)
+            nc.vector.tensor_tensor(
+                out=grouped[:].rearrange("p (c e i) -> p c i e", e=2, i=PACK),
+                in0=x1[u].rearrange("p i (c e) -> p c i e", e=2),
+                in1=weight.unsqueeze(2).to_broadcast([P, HALF // 2, PACK, 2]),
+                op=MULT,
+            )
+            return grouped
 
         def open_y(c):
             turned = bank("shift_ps%d" % c)
@@ -311,69 +310,96 @@ def tile_list_dome_patch_corrections_kernel(
                 )
             return y_ps
 
-        def proposals(c, z, w):
-            codes, scales, width = z
-            e4 = bank("e4_%d" % c)
-            e5 = bank("e5_%d" % c)
-            cols = [slice(width * a + P * w, width * a + P * (w + 1)) for a in range(2)]
-            for a in range(2):
-                nc.tensor.matmul_mx(
-                    out=e4[:], lhsT=codes[:, cols[a]].bitcast(FP8X4), lhsT_scale=scales[:, cols[a]],
-                    rhs=w4_codes[:, a, :].bitcast(FP4X4), rhs_scale=w4_scale[:, a, :],
-                    start=(a == 0), stop=(a == 1),
-                )
-            for a in range(2):
-                nc.tensor.matmul_mx(
-                    out=e5[:], lhsT=codes[:, cols[a]].bitcast(FP8X4), lhsT_scale=scales[:, cols[a]],
-                    rhs=w5_planes[a][0][:].bitcast(FP8X4), rhs_scale=w5_planes[a][1][:],
-                    start=(a == 0), stop=(a == 1),
-                )
-            e4_sb = ring.tile([P, N], F32, name="e4_sb%d" % c, tag="e4_sb", bufs=2)
+        def second_pass(sums, z, w, a):
+            codes, scales = z
+            cols = slice(P * w, P * (w + 1))
+            nc.tensor.matmul_mx(
+                out=sums[0][:], lhsT=codes[:, cols].bitcast(FP8X4), lhsT_scale=scales[:, cols],
+                rhs=w4_codes[:, a, :].bitcast(FP4X4), rhs_scale=w4_scale[:, a, :],
+                start=(a == 0), stop=(a == 1),
+            )
+            nc.tensor.matmul_mx(
+                out=sums[1][:], lhsT=codes[:, cols].bitcast(FP8X4), lhsT_scale=scales[:, cols],
+                rhs=w5_planes[a][0][:].bitcast(FP8X4), rhs_scale=w5_planes[a][1][:],
+                start=(a == 0), stop=(a == 1),
+            )
+
+        def open_sums(u):
+            z = z_upper(u)
+            sums = [(bank("e4_%d" % c), bank("e5_%d" % c)) for c in (2 * u, 2 * u + 1)]
+            for w in range(2):
+                second_pass(sums[w], z, w, 0)
+            return sums
+
+        def proposals(c, sums, e4_sb):
+            e4, e5 = sums
             nc.scalar.copy(
-                out=e4_sb[:].rearrange("m (i p) -> m i p", i=PACK),
+                out=e4_sb.rearrange("m (i p) -> m i p", i=PACK),
                 in_=e4[:].rearrange("m (p i) -> m i p", i=PACK),
             )
-            larger = ring.tile([P, N], F32, name="larger%d" % c, tag="larger", bufs=3)
-            nc.vector.tensor_tensor(out=larger[:], in0=e5[:], in1=e4_sb[:], op=MAX)
+            larger = ring.tile([P, N], F32, name="larger%d" % c, tag="larger", bufs=4)
+            nc.vector.tensor_tensor(out=larger[:], in0=e5[:], in1=e4_sb, op=MAX)
             return larger
 
-        def close_y(y_ps, larger, y, w):
+        def close_y(y_ps, larger):
             for i in range(PACK):
                 cols = slice(P * i, P * (i + 1))
                 nc.tensor.matmul(
                     y_ps[:, cols], larger[:, cols], ident[:], start=False, stop=(i == PACK - 1), is_transpose=True
                 )
-            nc.scalar.copy(out=y[:, :, P * w : P * (w + 1)], in_=y_ps[:].rearrange("p (i m) -> p i m", i=PACK))
 
-        def place(s, y, store):
-            m0, width = pieces[s]
-            for i in range(PACK):
-                nc.vector.tensor_tensor(
-                    out=pages[i][:].indirect(idx3[:, m0 // 16 : (m0 + width) // 16]),
-                    in0=y[:, i, :],
-                    in1=wgo_sb[:, m0 : m0 + width],
-                    op=MULT,
-                )
-                if store:
-                    nc.sync.dma_start(out=rows4(out, 0, 0, T2)[:, i, :], in_=pages[i][:])
+        def empty_y(y_ps, y, w, i0):
+            rows = y.shape[1]
+            nc.scalar.copy(
+                out=y[:, :, P * w : P * (w + 1)],
+                in_=y_ps[:].rearrange("p (i m) -> p i m", i=PACK)[:, i0 : i0 + rows, :],
+            )
 
-        ys = [placed([P, PACK, width], F32, "y%d" % s, 56 + m0 // 64) for s, (m0, width) in enumerate(pieces)]
-        x1 = gather1(0, weigh1(0, P), 0)
+        def place(u, i, y):
+            nc.vector.tensor_tensor(
+                out=pages[i][:].indirect(idx3[:, 16 * u : 16 * (u + 1)]),
+                in0=y,
+                in1=wgo_sb[:, HALF * u : HALF * (u + 1)],
+                op=MULT,
+            )
+
+        for i in range(PACK):
+            gather1(0, i)
         w5_operand(1, "vector")
-        z = z_operand(0, x1)
-        y_ps0 = open_y(0)
-        larger0 = proposals(0, z, 0)
-        close_y(y_ps0, larger0, ys[0], 0)
-        factor = weigh1(P, rest)
-        z = z_operand(1, gather1(1, factor, P))
-        y_ps1 = open_y(1)
-        larger1 = proposals(1, z, 0)
-        z = z_operand(2, gather1(2, factor, P))
-        place(0, ys[0], False)
-        larger2 = proposals(2, z, 0)
-        larger3 = proposals(3, z, 1)
-        close_y(y_ps1, larger1, ys[1], 0)
-        close_y(open_y(2), larger2, ys[2], 0)
-        close_y(open_y(3), larger3, ys[2], 1)
-        place(1, ys[1], False)
-        place(2, ys[2], True)
+        sums = open_sums(0)
+        grouped = z_lower_rows(0)
+        gather1(1, 0)
+        z = z_operand("z1_0", grouped)
+        for w in range(2):
+            second_pass(sums[w], z, w, 1)
+        gather1(1, 1)
+        gather1(1, 2)
+        e4_first = [placed([P, N], F32, "e4_sb0", 76)[:], x1_bytes[:, PACK * HALF : PACK * ROW]]
+        larger = [proposals(c, sums[c], e4_first[c]) for c in range(2)]
+        gather1(1, 3)
+        y_ps = []
+        y_first = placed([P, 2, HALF], F32, "y_first", 56)
+        for c in range(2):
+            y_ps.append(open_y(c))
+            close_y(y_ps[c], larger[c])
+            empty_y(y_ps[c], y_first, c, 0)
+        sums = open_sums(1)
+        z = z_operand("z1_1", z_lower_rows(1))
+        for w in range(2):
+            second_pass(sums[w], z, w, 1)
+        larger = [proposals(2 + w, sums[w], placed([P, N], F32, "e4_sb%d" % (2 + w), 72 + 2 * w)[:]) for w in range(2)]
+        for i in range(2):
+            place(0, i, y_first[:, i, :])
+        y_second = placed([P, 2, HALF], F32, "y_second", 72)
+        for c in range(2):
+            empty_y(y_ps[c], y_second, c, 2)
+        y_last = placed([P, PACK, HALF], F32, "y_last", 60)
+        for w in range(2):
+            y_bank = open_y(2 + w)
+            close_y(y_bank, larger[w])
+            empty_y(y_bank, y_last, w, 0)
+        for i in range(2):
+            place(0, 2 + i, y_second[:, i, :])
+        for i in range(PACK):
+            place(1, i, y_last[:, i, :])
+            nc.sync.dma_start(out=rows4(out, 0, 0, T2)[:, i, :], in_=pages[i][:])

@@ -21,9 +21,26 @@ IDENTITY = mybir.ActivationFunctionType.Identity
 P = 128
 PACK = 4
 PASS = P * PACK
+K_PASSES = K // PASS
 BANK = 512
-HALF = 256
-ROW = 384
+HALF = M // 2
+GROUP = 16
+QUADRANTS = 4
+SLOT = 1024
+EARLY_PLANES = 2
+
+TAB_AT = (0, 16, 32)
+W1_AT = {(1, 1): 0, (2, 1): 8, (0, 0): 48, (1, 0): 56, (0, 1): 64}
+W5_AT = (16, 32)
+VIEW1_AT = 24
+SHIFT_AT = 40
+X1_AT = 48
+Z0_AT = (64, 66)
+Z1_AT = (68, 70)
+E4_AT = {0: 76, 2: 72, 3: 74}
+Y_LATE_AT = 72
+Y_SECOND_AT = 80
+Y_EARLY_AT = 84
 
 
 def tile_list_dome_patch_corrections_kernel(
@@ -44,19 +61,16 @@ def tile_list_dome_patch_corrections_kernel(
         def placed(shape, dtype, name, kib):
             return arena.tile(shape, dtype, name=name, align_bytes=64, offset=1024 * kib)
 
-        def round_copy(engine, dst, src):
-            if engine == "vector":
-                nc.vector.tensor_copy(out=dst, in_=src)
-            else:
-                nc.scalar.copy(out=dst, in_=src)
+        def rows4(matrix, r0, c0, width):
+            return matrix[r0 : r0 + PASS, c0 : c0 + width].rearrange("(p j) c -> p j c", j=PACK)
 
-        def deal_round(engine, grouped, raw, m0):
-            width = raw.shape[2] // PACK
-            dst = grouped.rearrange("p (t m j) -> p m j t", t=PACK, j=PACK)[:, m0 : m0 + width, :, :]
-            round_copy(engine, dst, raw[:].rearrange("p j (m t) -> p m j t", t=PACK))
+        def deal_round(copy, rounded, raw, n0):
+            count = raw.shape[2] // PACK
+            dealt = rounded.rearrange("p (i n j) -> p n j i", i=PACK, j=PACK)
+            copy(out=dealt[:, n0 : n0 + count, :, :], in_=raw[:].rearrange("p j (n i) -> p n j i", i=PACK))
 
-        def quantise(codes, scales, grouped):
-            nc.vector.quantize_mx(out=codes.bitcast(FP8X4), scales=scales, in_=grouped)
+        def quantise(codes, scales, rounded):
+            nc.vector.quantize_mx(out=codes.bitcast(FP8X4), scales=scales, in_=rounded)
 
         tab_scale = keep.tile([P, T], U8, name="tab_scale", align_bytes=64)
         nc.vector.memset(tab_scale[:].bitcast(I32), 0)
@@ -70,233 +84,263 @@ def tile_list_dome_patch_corrections_kernel(
         ident = keep.tile([P, P], F32, name="ident")
         make_identity(nc, ident[:])
 
-        idx = lists.tile([P, S // 16], U16, name="idx")
-        idx2 = lists.tile([P, M // 16], U16, name="idx2")
-        idx3 = lists.tile([P, M // 16], U16, name="idx3")
+        idx = lists.tile([P, S // GROUP], U16, name="idx")
+        idx2 = lists.tile([P, M // GROUP], U16, name="idx2")
+        idx3 = lists.tile([P, M // GROUP], U16, name="idx3")
 
         def load_table(a):
-            words = placed([P, T], U32, "tab%d" % a, 16 * a)
+            words = placed([P, T], U32, "tab%d" % a, TAB_AT[a])
             nc.sync.dma_start(
                 out=words[:].bitcast(I32),
-                in_=tab_words[a].rearrange("p t i -> p (t i)").bitcast(I32),
+                in_=tab_words[a].rearrange("p t j -> p (t j)").bitcast(I32),
             )
             return words
 
-        def rows4(matrix, r0, c0, width):
-            return matrix[r0 : r0 + PASS, c0 : c0 + width].rearrange("(p j) c -> p j c", j=PACK)
-
-        def load_w1(a, b, kib):
-            raw = placed([P, PACK, PASS], F32, "w1raw%d%d" % (a, b), kib)
+        def load_w1(a, b):
+            raw = placed([P, PACK, PASS], F32, "w1raw%d%d" % (a, b), W1_AT[(a, b)])
             nc.sync.dma_start(out=raw[:], in_=rows4(w1, PASS * a, PASS * b, PASS))
             return raw
 
-        def load_view0(u):
-            factor = keep.tile([P, 2, M], F32, name="view0%d" % u)
-            nc.sync.dma_start(out=factor[:], in_=rows4(view, 0, 0, M)[:, 2 * u : 2 * u + 2, :])
+        def load_view0(pair):
+            factor = keep.tile([P, 2, M], F32, name="view0%d" % pair)
+            nc.sync.dma_start(out=factor[:], in_=rows4(view, 0, 0, M)[:, 2 * pair : 2 * pair + 2, :])
             return factor
 
         nc.sync.dma_start(idx[:], offs)
         tab = [load_table(0)]
-        for q in range(4):
-            nc.sync.dma_start(
-                out=tab_scale[32 * q : 32 * q + 12, :].bitcast(I32),
-                in_=tab_scales[:, 4 * q : 4 * q + 4, :].bitcast(I32),
+        for quad in range(QUADRANTS):
+            nc.gpsimd.dma_start(
+                out=tab_scale[32 * quad : 32 * quad + 4 * K_PASSES, :].bitcast(I32),
+                in_=tab_scales[:, 4 * quad : 4 * quad + 4, :].bitcast(I32),
             )
-        w1_raw = {(0, 0): load_w1(0, 0, 48)}
+        w1_raw = {(0, 0): load_w1(0, 0)}
+        tab.append(load_table(1))
+        w1_raw[(1, 0)] = load_w1(1, 0)
+        tab.append(load_table(2))
         nc.sync.dma_start(idx2[:], offs2)
         nc.sync.dma_start(out=bias[:], in_=b1.rearrange("(b p i) -> p b i", b=2, i=PACK))
-        tab.append(load_table(1))
-        w1_raw[(1, 0)] = load_w1(1, 0, 56)
-        tab.append(load_table(2))
+        side_width = PASS // 2
         last_raw = []
-        for u in range(2):
-            raw = keep.tile([P, PACK, HALF], F32, name="w1last%d" % u)
-            nc.sync.dma_start(out=raw[:], in_=rows4(w1, PASS * 2, HALF * u, HALF))
+        for side in range(2):
+            raw = keep.tile([P, PACK, side_width], F32, name="w1last%d" % side)
+            nc.sync.dma_start(out=raw[:], in_=rows4(w1, PASS * (K_PASSES - 1), side_width * side, side_width))
             last_raw.append(raw)
         wgt_sb = keep.tile([P, M], F32, name="wgt_sb")
         nc.sync.dma_start(out=wgt_sb[:], in_=wgt)
         view0 = [load_view0(0)]
-        w1_raw[(0, 1)] = load_w1(0, 1, 64)
+        w1_raw[(0, 1)] = load_w1(0, 1)
         view0.append(load_view0(1))
 
         v_codes = []
         v_scale = keep.tile([P, S], U8, name="v_scale", align_bytes=64)
-        for a in range(3):
+        for a in range(K_PASSES):
             picked = keep.tile([P, S], U32, name="v_codes%d" % a, align_bytes=64)
             nc.vector.tensor_copy(out=picked[:], in_=tab[a][:].indirect(idx[:]))
             v_codes.append(picked)
             if a == 0:
                 nc.vector.tensor_copy(out=v_scale[:], in_=tab_scale[:].indirect(idx[:]))
 
-        def grouped_tile(name):
-            return ring.tile([P, PASS * PACK], BF16, name=name, tag="grouped", bufs=3, align_bytes=64)
+        def rounded_tile(name):
+            return ring.tile([P, PASS * PACK], BF16, name=name, tag="rounded", bufs=3, align_bytes=64)
 
-        def w1_planes(a, b):
+        def w1_tiles(a, b):
             codes = ring.tile([P, PASS], U32, name="w1c%d%d" % (a, b), tag="w1c", bufs=4, align_bytes=64)
             scales = ring.tile([P, PASS], U8, name="w1s%d%d" % (a, b), tag="w1s", bufs=4, align_bytes=64)
             return codes, scales
 
-        def first_pass(acc, planes, a, i, start, stop):
-            codes, scales = planes
+        def w1_operand(a, b, copy, rounded):
+            deal_round(copy, rounded, w1_raw[(a, b)], 0)
+            codes, scales = w1_tiles(a, b)
+            quantise(codes[:], scales[:], rounded)
+            return codes, scales
+
+        def h_banks(b):
+            return [[bank("h%d_%d%d" % (b, i, part)) for part in range(S // BANK)] for i in range(PACK)]
+
+        def h_pass(banks, w1_mx, a, i, start, stop):
+            codes, scales = w1_mx
             cols = slice(P * i, P * (i + 1))
-            for u in range(2):
-                entries = slice(BANK * u, BANK * (u + 1))
+            for part in range(S // BANK):
+                listed = slice(BANK * part, BANK * (part + 1))
                 nc.tensor.matmul_mx(
-                    out=acc[i][u][:],
+                    out=banks[i][part][:],
                     lhsT=codes[:, cols].bitcast(FP8X4),
                     lhsT_scale=scales[:, cols],
-                    rhs=v_codes[a][:, entries].bitcast(FP8X4),
-                    rhs_scale=v_scale[4 * a : P, entries],
+                    rhs=v_codes[a][:, listed].bitcast(FP8X4),
+                    rhs_scale=v_scale[4 * a : P, listed],
                     start=start,
                     stop=stop,
                 )
 
-        def empty_h(acc, b, i):
-            h = ring.tile([P, S], F32, name="h%d%d" % (b, i), tag="h", bufs=8)
-            for u in range(2):
+        def empty_h(banks, b, i):
+            h = ring.tile([P, S], F32, name="h%d%d" % (b, i), tag="h", bufs=2 * PACK)
+            for part in range(S // BANK):
                 nc.scalar.activation(
-                    out=h[:, BANK * u : BANK * (u + 1)], in_=acc[i][u][:], func=IDENTITY,
+                    out=h[:, BANK * part : BANK * (part + 1)], in_=banks[i][part][:], func=IDENTITY,
                     bias=bias[:, b, i : i + 1],
                 )
             return h
 
-        def interleave(grouped, picked):
-            nc.scalar.copy(
-                out=grouped.rearrange("p (c e i) -> p c i e", e=4, i=PACK),
-                in_=picked.rearrange("p i (c e) -> p c i e", e=4),
-            )
-
-        acc0 = [[bank("h0_%d%d" % (i, u)) for u in range(2)] for i in range(PACK)]
-        for a in range(2):
-            grouped = grouped_tile("g%d0" % a)
-            deal_round("scalar", grouped[:], w1_raw[(a, 0)], 0)
-            planes = w1_planes(a, 0)
-            quantise(planes[0][:], planes[1][:], grouped[:])
+        banks0 = h_banks(0)
+        for a in range(K_PASSES - 1):
+            w1_mx = w1_operand(a, 0, nc.scalar.copy, rounded_tile("w1r%d0" % a)[:])
             for i in range(PACK):
-                first_pass(acc0, planes, a, i, a == 0, False)
-        w1_raw[(1, 1)] = load_w1(1, 1, 0)
-        w1_raw[(2, 1)] = load_w1(2, 1, 8)
+                h_pass(banks0, w1_mx, a, i, a == 0, False)
 
-        def load_w5(a):
-            raw = placed([P, PACK, N], F32, "w5raw%d" % a, 16 + 16 * a)
-            nc.sync.dma_start(out=raw[:], in_=rows4(w5, PASS * a, 0, N))
+        def load_w5(b):
+            raw = placed([P, PACK, N], F32, "w5raw%d" % b, W5_AT[b])
+            nc.sync.dma_start(out=raw[:], in_=rows4(w5, PASS * b, 0, N))
             return raw
 
+        w1_raw[(1, 1)] = load_w1(1, 1)
+        w1_raw[(2, 1)] = load_w1(2, 1)
         w5_raw = [load_w5(0)]
-        view1 = placed([P, PACK, M], F32, "view1", 24)
+        view1 = placed([P, PACK, M], F32, "view1", VIEW1_AT)
         nc.sync.dma_start(out=view1[:], in_=rows4(view, PASS, 0, M))
         w5_raw.append(load_w5(1))
-        shift_sb = placed([P, PACK, M], F32, "shift_sb", 40)
+        shift_sb = placed([P, PACK, M], F32, "shift_sb", SHIFT_AT)
         nc.sync.dma_start(out=shift_sb[:], in_=rows4(shift, 0, 0, M))
         w4_codes = keep.tile([P, 2, 2 * N], U8, name="w4_codes", align_bytes=64)
         nc.sync.dma_start(
-            out=w4_codes[:].bitcast(I32), in_=w4_words.rearrange("a p c -> p a c").bitcast(I32)
+            out=w4_codes[:].bitcast(I32), in_=w4_words.rearrange("b p c -> p b c").bitcast(I32)
         )
-        for q in range(4):
+        for quad in range(QUADRANTS):
             nc.sync.dma_start(
-                out=w4_scale[32 * q : 32 * q + 4, :, :].bitcast(I32),
-                in_=w4_scales[:, 4 * q : 4 * q + 4, :].rearrange("a r c -> r a c").bitcast(I32),
+                out=w4_scale[32 * quad : 32 * quad + 4, :, :].bitcast(I32),
+                in_=w4_scales[:, 4 * quad : 4 * quad + 4, :].rearrange("b r c -> r b c").bitcast(I32),
             )
         wgo_sb = keep.tile([P, M], F32, name="wgo_sb")
         nc.sync.dma_start(out=wgo_sb[:], in_=wgo)
         nc.sync.dma_start(idx3[:], offs3)
 
-        grouped = grouped_tile("g20")
-        deal_round("scalar", grouped[:], last_raw[0], 0)
-        deal_round("vector", grouped[:], last_raw[1], HALF // PACK)
-        planes = w1_planes(2, 0)
+        rounded = rounded_tile("w1r20")
+        deal_round(nc.scalar.copy, rounded[:], last_raw[0], 0)
+        deal_round(nc.vector.tensor_copy, rounded[:], last_raw[1], side_width // PACK)
+        w1_mx = w1_tiles(K_PASSES - 1, 0)
         for i in range(PACK):
             cols = slice(P * i, P * (i + 1))
-            quantise(planes[0][:, cols], planes[1][:, cols], grouped[:, PASS * i : PASS * (i + 1)])
-            first_pass(acc0, planes, 2, i, False, True)
+            quantise(w1_mx[0][:, cols], w1_mx[1][:, cols], rounded[:, PASS * i : PASS * (i + 1)])
+            h_pass(banks0, w1_mx, K_PASSES - 1, i, False, True)
 
-        x0_bytes = keep.tile([P, PACK * 2 * M], F32, name="x0", align_bytes=64)
-        x0 = x0_bytes[:].rearrange("p (i m) -> p i m", i=PACK)[:, :, 0:M]
+        z0_bytes = keep.tile([P, (PACK + 1) * M], F32, name="z0", align_bytes=64)
+        z0 = z0_bytes[:, 0 : PACK * M].rearrange("p (i m) -> p i m", i=PACK)
 
-        def pick0(i):
-            h = empty_h(acc0, 0, i)
-            row = view0[i // 2][:, i % 2, :]
-            nc.vector.tensor_tensor(out=row, in0=row, in1=wgt_sb[:], op=MULT)
-            return h, row
+        def prepare0(i):
+            h = empty_h(banks0, 0, i)
+            pair = view0[i // 2]
+            if i % 2 == 0:
+                nc.vector.tensor_tensor(
+                    out=pair[:], in0=pair[:], in1=wgt_sb[:].unsqueeze(1).to_broadcast([P, 2, M]), op=MULT
+                )
+            return h, pair[:, i % 2, :]
 
-        def gather0(i, h, row):
-            nc.vector.tensor_tensor(
-                out=x0[:, i, :], in0=h[:].indirect(idx2[:]), in1=row, op=MULT
-            )
+        def gather0(i, h, factor):
+            nc.vector.tensor_tensor(out=z0[:, i, :], in0=h[:].indirect(idx2[:]), in1=factor, op=MULT)
 
-        acc1 = [[bank("h1_%d%d" % (i, u)) for u in range(2)] for i in range(PACK)]
-
-        def w1_second(a, engine, grouped):
-            deal_round(engine, grouped, w1_raw[(a, 1)], 0)
-            planes = w1_planes(a, 1)
-            quantise(planes[0][:], planes[1][:], grouped)
-            return planes
-
-        gather0(0, *pick0(0))
-        gather0(1, *pick0(1))
-        planes = w1_second(0, "scalar", grouped_tile("g01")[:])
-        gather0(2, *pick0(2))
-        held = pick0(3)
+        banks1 = h_banks(1)
+        gather0(0, *prepare0(0))
+        gather0(1, *prepare0(1))
+        w1_mx0 = w1_operand(0, 1, nc.scalar.copy, rounded_tile("w1r01")[:])
+        gather0(2, *prepare0(2))
+        last_plane = prepare0(3)
         for i in range(PACK):
-            first_pass(acc1, planes, 0, i, True, False)
-        planes2 = w1_second(2, "vector", grouped_tile("g21")[:])
-        planes1 = w1_second(1, "scalar", x0_bytes[:, 6 * M : 8 * M].bitcast(BF16))
-        gather0(3, *held)
+            h_pass(banks1, w1_mx0, 0, i, True, False)
+        w1_mx2 = w1_operand(2, 1, nc.vector.tensor_copy, rounded_tile("w1r21")[:])
+        w1_mx1 = w1_operand(1, 1, nc.scalar.copy, z0_bytes[:, (PACK - 1) * M : (PACK + 1) * M].bitcast(BF16))
+        gather0(3, *last_plane)
 
-        w5_planes = []
+        w5_mx = []
 
-        def w5_operand(a, engine):
-            grouped = grouped_tile("g5%d" % a)
-            deal_round(engine, grouped[:], w5_raw[a], 0)
-            codes = keep.tile([P, N], U32, name="w5c%d" % a, align_bytes=64)
-            scales = keep.tile([P, N], U8, name="w5s%d" % a, align_bytes=64)
-            quantise(codes[:], scales[:], grouped[:])
-            w5_planes.append((codes, scales))
+        def w5_operand(b, rounded):
+            deal_round(nc.scalar.copy, rounded, w5_raw[b], 0)
+            codes = keep.tile([P, N], U32, name="w5c%d" % b, align_bytes=64)
+            scales = keep.tile([P, N], U8, name="w5s%d" % b, align_bytes=64)
+            quantise(codes[:], scales[:], rounded)
+            w5_mx.append((codes, scales))
 
         h1 = []
         for i in range(PACK):
-            first_pass(acc1, planes2, 2, i, False, False)
-            first_pass(acc1, planes1, 1, i, False, True)
-            h1.append(empty_h(acc1, 1, i))
-        w5_operand(0, "scalar")
+            h_pass(banks1, w1_mx2, 2, i, False, False)
+            h_pass(banks1, w1_mx1, 1, i, False, True)
+            h1.append(empty_h(banks1, 1, i))
+        w5_operand(0, rounded_tile("w5r0")[:])
 
-        x1_bytes = placed([P, PACK * ROW], F32, "x1", 48)
+        x1_bytes = placed([P, PACK * SLOT], F32, "x1", X1_AT)
         x1 = (
-            x1_bytes[:, 0 : PACK * HALF].rearrange("p (i m) -> p i m", i=PACK),
+            x1_bytes[:, SLOT : 2 * SLOT].rearrange("p (i m) -> p i m", i=PACK),
             x1_bytes[:].rearrange("p (i m) -> p i m", i=PACK)[:, :, 0:HALF],
         )
+
+        def list_half(entries, u):
+            return entries[:, HALF // GROUP * u : HALF // GROUP * (u + 1)]
 
         def gather1(u, i):
             nc.vector.tensor_tensor(
                 out=x1[u][:, i, :],
-                in0=h1[i][:].indirect(idx2[:, 16 * u : 16 * (u + 1)]),
+                in0=h1[i][:].indirect(list_half(idx2, u)),
                 in1=view1[:, i, HALF * u : HALF * (u + 1)],
                 op=MULT,
             )
 
-        def z_operand(name, grouped):
-            codes = keep.tile([P, HALF], U32, name="%s_codes" % name, align_bytes=64)
-            scales = keep.tile([P, HALF], U8, name="%s_scale" % name, align_bytes=64)
-            quantise(codes[:], scales[:], grouped[:])
-            return codes, scales
+        def round_z0(u):
+            rounded = placed([P, PACK * HALF], BF16, "z0r%d" % u, Z0_AT[u])
+            nc.scalar.copy(
+                out=rounded[:].rearrange("p (s e i) -> p s i e", e=4, i=PACK),
+                in_=z0[:, :, HALF * u : HALF * (u + 1)].rearrange("p i (s e) -> p s i e", e=4),
+            )
+            return rounded
 
-        def z_upper(u):
-            grouped = placed([P, PACK * HALF], BF16, "gz0_%d" % u, 64 + 2 * u)
-            interleave(grouped[:], x0[:, :, HALF * u : HALF * (u + 1)])
-            return z_operand("z0_%d" % u, grouped)
-
-        def z_lower_rows(u):
-            grouped = placed([P, PACK * HALF], BF16, "gz1_%d" % u, 68 + 2 * u)
-            weight = wgt_sb[:, HALF * u : HALF * (u + 1)].rearrange("p (c e) -> p c e", e=2)
+        def round_z1(u):
+            rounded = placed([P, PACK * HALF], BF16, "z1r%d" % u, Z1_AT[u])
+            weight = wgt_sb[:, HALF * u : HALF * (u + 1)].rearrange("p (s e) -> p s e", e=2)
             nc.vector.tensor_tensor(
-                out=grouped[:].rearrange("p (c e i) -> p c i e", e=2, i=PACK),
-                in0=x1[u].rearrange("p i (c e) -> p c i e", e=2),
+                out=rounded[:].rearrange("p (s e i) -> p s i e", e=2, i=PACK),
+                in0=x1[u].rearrange("p i (s e) -> p s i e", e=2),
                 in1=weight.unsqueeze(2).to_broadcast([P, HALF // 2, PACK, 2]),
                 op=MULT,
             )
-            return grouped
+            return rounded
 
-        def open_y(c):
+        def z_operand(b, u, rounded):
+            codes = keep.tile([P, HALF], U32, name="z%d%d_codes" % (b, u), align_bytes=64)
+            scales = keep.tile([P, HALF], U8, name="z%d%d_scale" % (b, u), align_bytes=64)
+            quantise(codes[:], scales[:], rounded[:])
+            return codes, scales
+
+        def sums_pass(sums, z_mx, b):
+            codes, scales = z_mx
+            for w, (e4, e5) in enumerate(sums):
+                cols = slice(P * w, P * (w + 1))
+                nc.tensor.matmul_mx(
+                    out=e4[:], lhsT=codes[:, cols].bitcast(FP8X4), lhsT_scale=scales[:, cols],
+                    rhs=w4_codes[:, b, :].bitcast(FP4X4), rhs_scale=w4_scale[:, b, :],
+                    start=(b == 0), stop=(b == 1),
+                )
+                nc.tensor.matmul_mx(
+                    out=e5[:], lhsT=codes[:, cols].bitcast(FP8X4), lhsT_scale=scales[:, cols],
+                    rhs=w5_mx[b][0][:].bitcast(FP8X4), rhs_scale=w5_mx[b][1][:],
+                    start=(b == 0), stop=(b == 1),
+                )
+
+        def open_sums(u):
+            z_mx = z_operand(0, u, round_z0(u))
+            sums = [(bank("e4_%d" % c), bank("e5_%d" % c)) for c in (2 * u, 2 * u + 1)]
+            sums_pass(sums, z_mx, 0)
+            return sums
+
+        def larger_of(c, e4, e5, e4_sb):
+            nc.scalar.copy(
+                out=e4_sb.rearrange("m (i p) -> m i p", i=PACK),
+                in_=e4[:].rearrange("m (p i) -> m i p", i=PACK),
+            )
+            larger = ring.tile([P, N], F32, name="larger%d" % c, tag="larger", bufs=M // P)
+            nc.vector.tensor_tensor(out=larger[:], in0=e5[:], in1=e4_sb, op=MAX)
+            return larger
+
+        def e4_tile(c):
+            return placed([P, N], F32, "e4_sb%d" % c, E4_AT[c])[:]
+
+        def y_bank(c, larger):
             turned = bank("shift_ps%d" % c)
             for i in range(PACK):
                 nc.tensor.transpose(turned[:, P * i : P * (i + 1)], shift_sb[:, i, P * c : P * (c + 1)], ident[:])
@@ -308,98 +352,60 @@ def tile_list_dome_patch_corrections_kernel(
                 nc.tensor.matmul(
                     y_ps[:, cols], shift_t[:, cols], ident[:], start=(i == 0), stop=False, is_transpose=True
                 )
-            return y_ps
-
-        def second_pass(sums, z, w, a):
-            codes, scales = z
-            cols = slice(P * w, P * (w + 1))
-            nc.tensor.matmul_mx(
-                out=sums[0][:], lhsT=codes[:, cols].bitcast(FP8X4), lhsT_scale=scales[:, cols],
-                rhs=w4_codes[:, a, :].bitcast(FP4X4), rhs_scale=w4_scale[:, a, :],
-                start=(a == 0), stop=(a == 1),
-            )
-            nc.tensor.matmul_mx(
-                out=sums[1][:], lhsT=codes[:, cols].bitcast(FP8X4), lhsT_scale=scales[:, cols],
-                rhs=w5_planes[a][0][:].bitcast(FP8X4), rhs_scale=w5_planes[a][1][:],
-                start=(a == 0), stop=(a == 1),
-            )
-
-        def open_sums(u):
-            z = z_upper(u)
-            sums = [(bank("e4_%d" % c), bank("e5_%d" % c)) for c in (2 * u, 2 * u + 1)]
-            for w in range(2):
-                second_pass(sums[w], z, w, 0)
-            return sums
-
-        def proposals(c, sums, e4_sb):
-            e4, e5 = sums
-            nc.scalar.copy(
-                out=e4_sb.rearrange("m (i p) -> m i p", i=PACK),
-                in_=e4[:].rearrange("m (p i) -> m i p", i=PACK),
-            )
-            larger = ring.tile([P, N], F32, name="larger%d" % c, tag="larger", bufs=4)
-            nc.vector.tensor_tensor(out=larger[:], in0=e5[:], in1=e4_sb, op=MAX)
-            return larger
-
-        def close_y(y_ps, larger):
             for i in range(PACK):
                 cols = slice(P * i, P * (i + 1))
                 nc.tensor.matmul(
                     y_ps[:, cols], larger[:, cols], ident[:], start=False, stop=(i == PACK - 1), is_transpose=True
                 )
+            return y_ps
 
         def empty_y(y_ps, y, w, i0):
-            rows = y.shape[1]
             nc.scalar.copy(
                 out=y[:, :, P * w : P * (w + 1)],
-                in_=y_ps[:].rearrange("p (i m) -> p i m", i=PACK)[:, i0 : i0 + rows, :],
+                in_=y_ps[:].rearrange("p (i m) -> p i m", i=PACK)[:, i0 : i0 + y.shape[1], :],
             )
 
-        def place(u, i, y):
+        def place(u, i, y_plane):
             nc.vector.tensor_tensor(
-                out=pages[i][:].indirect(idx3[:, 16 * u : 16 * (u + 1)]),
-                in0=y,
+                out=pages[i][:].indirect(list_half(idx3, u)),
+                in0=y_plane,
                 in1=wgo_sb[:, HALF * u : HALF * (u + 1)],
                 op=MULT,
             )
 
-        for i in range(PACK):
-            gather1(0, i)
-        w5_operand(1, "vector")
-        sums = open_sums(0)
-        grouped = z_lower_rows(0)
+        gather1(0, 0)
         gather1(1, 0)
-        z = z_operand("z1_0", grouped)
-        for w in range(2):
-            second_pass(sums[w], z, w, 1)
+        for i in range(1, PACK):
+            gather1(0, i)
+        sums = open_sums(0)
+        rounded = round_z1(0)
         gather1(1, 1)
+        z_mx = z_operand(1, 0, rounded)
+        w5_operand(1, x1_bytes[:, 2 * SLOT : 3 * SLOT].bitcast(BF16))
+        sums_pass(sums, z_mx, 1)
         gather1(1, 2)
-        e4_first = [placed([P, N], F32, "e4_sb0", 76)[:], x1_bytes[:, PACK * HALF : PACK * ROW]]
-        larger = [proposals(c, sums[c], e4_first[c]) for c in range(2)]
+        e4_first = (e4_tile(0), x1_bytes[:, 3 * SLOT : 3 * SLOT + N])
+        larger = [larger_of(c, *sums[c], e4_first[c]) for c in range(2)]
         gather1(1, 3)
-        y_ps = []
-        y_first = placed([P, 2, HALF], F32, "y_first", 56)
+        y_first = []
+        y_early = placed([P, EARLY_PLANES, HALF], F32, "y_early", Y_EARLY_AT)
         for c in range(2):
-            y_ps.append(open_y(c))
-            close_y(y_ps[c], larger[c])
-            empty_y(y_ps[c], y_first, c, 0)
+            y_first.append(y_bank(c, larger[c]))
+            empty_y(y_first[c], y_early, c, 0)
+
         sums = open_sums(1)
-        z = z_operand("z1_1", z_lower_rows(1))
-        for w in range(2):
-            second_pass(sums[w], z, w, 1)
-        larger = [proposals(2 + w, sums[w], placed([P, N], F32, "e4_sb%d" % (2 + w), 72 + 2 * w)[:]) for w in range(2)]
-        for i in range(2):
-            place(0, i, y_first[:, i, :])
-        y_second = placed([P, 2, HALF], F32, "y_second", 72)
+        sums_pass(sums, z_operand(1, 1, round_z1(1)), 1)
+        larger = [larger_of(2 + w, *sums[w], e4_tile(2 + w)) for w in range(2)]
+        for i in range(EARLY_PLANES):
+            place(0, i, y_early[:, i, :])
+        y_late = placed([P, PACK - EARLY_PLANES, HALF], F32, "y_late", Y_LATE_AT)
         for c in range(2):
-            empty_y(y_ps[c], y_second, c, 2)
-        y_last = placed([P, PACK, HALF], F32, "y_last", 60)
+            empty_y(y_first[c], y_late, c, EARLY_PLANES)
+        y_second = placed([P, PACK, HALF], F32, "y_second", Y_SECOND_AT)
         for w in range(2):
-            y_bank = open_y(2 + w)
-            close_y(y_bank, larger[w])
-            empty_y(y_bank, y_last, w, 0)
-        for i in range(2):
-            place(0, 2 + i, y_second[:, i, :])
+            empty_y(y_bank(2 + w, larger[w]), y_second, w, 0)
+        for i in range(EARLY_PLANES, PACK):
+            place(0, i, y_late[:, i - EARLY_PLANES, :])
         for i in range(PACK):
-            place(1, i, y_last[:, i, :])
+            place(1, i, y_second[:, i, :])
             nc.sync.dma_start(out=rows4(out, 0, 0, T2)[:, i, :], in_=pages[i][:])

from contextlib import ExitStack

import concourse.mybir as mybir
from concourse.masks import make_identity

K, T, S, H, M, N, T2 = 1536, 4096, 1024, 1024, 512, 512, 1024
FLOPS = 2 * K * H * S + 2 * 2 * H * N * M

F32 = mybir.dt.float32
BF16 = mybir.dt.bfloat16
I32 = mybir.dt.int32
U32 = mybir.dt.uint32
U16 = mybir.dt.uint16
U8 = mybir.dt.uint8
FP8X4 = mybir.dt.float8_e4m3fn_x4
FP4X4 = mybir.dt.float4_e2m1fn_x4
MULT = mybir.AluOpType.mult
MAX = mybir.AluOpType.max
IDENTITY = mybir.ActivationFunctionType.Identity

P = 128
PACK = 4
PASS = P * PACK
K_PASSES = K // PASS
BANK = 512
HALF = M // 2
GROUP = 16
QUADRANTS = 4
SLOT = 1024
EARLY_PLANES = 2

TAB_AT = (0, 16, 32)
W1_AT = {(1, 1): 0, (2, 1): 8, (0, 0): 48, (1, 0): 56, (0, 1): 64}
W5_AT = (16, 32)
VIEW1_AT = 24
SHIFT_AT = 40
X1_AT = 48
Z0_AT = (64, 66)
Z1_AT = (68, 70)
E4_AT = {0: 76, 2: 72, 3: 74}
Y_LATE_AT = 72
Y_SECOND_AT = 80
Y_EARLY_AT = 84


def tile_list_dome_patch_corrections_kernel(
    tc, tab_words, tab_scales, offs, w1, b1, offs2, wgt, view,
    w4_words, w4_scales, w5, shift, offs3, wgo, out,
):
    nc = tc.nc
    with ExitStack() as ctx:
        lists = ctx.enter_context(tc.tile_pool(name="lists", bufs=1))
        keep = ctx.enter_context(tc.tile_pool(name="keep", bufs=1))
        ring = ctx.enter_context(tc.tile_pool(name="ring", bufs=1))
        arena = ctx.enter_context(tc.tile_pool(name="arena", bufs=1))
        psum = ctx.enter_context(tc.psum_pool(name="psum", bufs=8))

        def bank(name):
            return psum.tile([P, BANK], F32, name=name, tag="bank")

        def placed(shape, dtype, name, kib):
            return arena.tile(shape, dtype, name=name, align_bytes=64, offset=1024 * kib)

        def rows4(matrix, r0, c0, width):
            return matrix[r0 : r0 + PASS, c0 : c0 + width].rearrange("(p j) c -> p j c", j=PACK)

        def deal_round(copy, rounded, raw, n0):
            count = raw.shape[2] // PACK
            dealt = rounded.rearrange("p (i n j) -> p n j i", i=PACK, j=PACK)
            copy(out=dealt[:, n0 : n0 + count, :, :], in_=raw[:].rearrange("p j (n i) -> p n j i", i=PACK))

        def quantise(codes, scales, rounded):
            nc.vector.quantize_mx(out=codes.bitcast(FP8X4), scales=scales, in_=rounded)

        tab_scale = keep.tile([P, T], U8, name="tab_scale", align_bytes=64)
        nc.vector.memset(tab_scale[:].bitcast(I32), 0)
        w4_scale = keep.tile([P, 2, N], U8, name="w4_scale", align_bytes=64)
        nc.vector.memset(w4_scale[:].bitcast(I32), 0)
        pages = [keep.tile([P, T2], F32, name="page%d" % i) for i in range(PACK)]
        for page in pages:
            nc.vector.memset(page[:], 0.0)

        bias = keep.tile([P, 2, PACK], F32, name="bias")
        ident = keep.tile([P, P], F32, name="ident")
        make_identity(nc, ident[:])

        idx = lists.tile([P, S // GROUP], U16, name="idx")
        idx2 = lists.tile([P, M // GROUP], U16, name="idx2")
        idx3 = lists.tile([P, M // GROUP], U16, name="idx3")

        def load_table(a):
            words = placed([P, T], U32, "tab%d" % a, TAB_AT[a])
            nc.sync.dma_start(
                out=words[:].bitcast(I32),
                in_=tab_words[a].rearrange("p t j -> p (t j)").bitcast(I32),
            )
            return words

        def load_w1(a, b):
            raw = placed([P, PACK, PASS], F32, "w1raw%d%d" % (a, b), W1_AT[(a, b)])
            nc.sync.dma_start(out=raw[:], in_=rows4(w1, PASS * a, PASS * b, PASS))
            return raw

        def load_view0(pair):
            factor = keep.tile([P, 2, M], F32, name="view0%d" % pair)
            nc.sync.dma_start(out=factor[:], in_=rows4(view, 0, 0, M)[:, 2 * pair : 2 * pair + 2, :])
            return factor

        nc.sync.dma_start(idx[:], offs)
        tab = [load_table(0)]
        for quad in range(QUADRANTS):
            nc.gpsimd.dma_start(
                out=tab_scale[32 * quad : 32 * quad + 4 * K_PASSES, :].bitcast(I32),
                in_=tab_scales[:, 4 * quad : 4 * quad + 4, :].bitcast(I32),
            )
        w1_raw = {(0, 0): load_w1(0, 0)}
        tab.append(load_table(1))
        w1_raw[(1, 0)] = load_w1(1, 0)
        tab.append(load_table(2))
        nc.sync.dma_start(idx2[:], offs2)
        nc.sync.dma_start(out=bias[:], in_=b1.rearrange("(b p i) -> p b i", b=2, i=PACK))
        side_width = PASS // 2
        last_raw = []
        for side in range(2):
            raw = keep.tile([P, PACK, side_width], F32, name="w1last%d" % side)
            nc.sync.dma_start(out=raw[:], in_=rows4(w1, PASS * (K_PASSES - 1), side_width * side, side_width))
            last_raw.append(raw)
        wgt_sb = keep.tile([P, M], F32, name="wgt_sb")
        nc.sync.dma_start(out=wgt_sb[:], in_=wgt)
        view0 = [load_view0(0)]
        w1_raw[(0, 1)] = load_w1(0, 1)
        view0.append(load_view0(1))

        v_codes = []
        v_scale = keep.tile([P, S], U8, name="v_scale", align_bytes=64)
        for a in range(K_PASSES):
            picked = keep.tile([P, S], U32, name="v_codes%d" % a, align_bytes=64)
            nc.vector.tensor_copy(out=picked[:], in_=tab[a][:].indirect(idx[:]))
            v_codes.append(picked)
            if a == 0:
                nc.vector.tensor_copy(out=v_scale[:], in_=tab_scale[:].indirect(idx[:]))

        def rounded_tile(name):
            return ring.tile([P, PASS * PACK], BF16, name=name, tag="rounded", bufs=3, align_bytes=64)

        def w1_tiles(a, b):
            codes = ring.tile([P, PASS], U32, name="w1c%d%d" % (a, b), tag="w1c", bufs=4, align_bytes=64)
            scales = ring.tile([P, PASS], U8, name="w1s%d%d" % (a, b), tag="w1s", bufs=4, align_bytes=64)
            return codes, scales

        def w1_operand(a, b, copy, rounded):
            deal_round(copy, rounded, w1_raw[(a, b)], 0)
            codes, scales = w1_tiles(a, b)
            quantise(codes[:], scales[:], rounded)
            return codes, scales

        def h_banks(b):
            return [[bank("h%d_%d%d" % (b, i, part)) for part in range(S // BANK)] for i in range(PACK)]

        def h_pass(banks, w1_mx, a, i, start, stop):
            codes, scales = w1_mx
            cols = slice(P * i, P * (i + 1))
            for part in range(S // BANK):
                listed = slice(BANK * part, BANK * (part + 1))
                nc.tensor.matmul_mx(
                    out=banks[i][part][:],
                    lhsT=codes[:, cols].bitcast(FP8X4),
                    lhsT_scale=scales[:, cols],
                    rhs=v_codes[a][:, listed].bitcast(FP8X4),
                    rhs_scale=v_scale[4 * a : P, listed],
                    start=start,
                    stop=stop,
                )

        def empty_h(banks, b, i):
            h = ring.tile([P, S], F32, name="h%d%d" % (b, i), tag="h", bufs=2 * PACK)
            for part in range(S // BANK):
                nc.scalar.activation(
                    out=h[:, BANK * part : BANK * (part + 1)], in_=banks[i][part][:], func=IDENTITY,
                    bias=bias[:, b, i : i + 1],
                )
            return h

        banks0 = h_banks(0)
        for a in range(K_PASSES - 1):
            w1_mx = w1_operand(a, 0, nc.scalar.copy, rounded_tile("w1r%d0" % a)[:])
            for i in range(PACK):
                h_pass(banks0, w1_mx, a, i, a == 0, False)

        def load_w5(b):
            raw = placed([P, PACK, N], F32, "w5raw%d" % b, W5_AT[b])
            nc.sync.dma_start(out=raw[:], in_=rows4(w5, PASS * b, 0, N))
            return raw

        w1_raw[(1, 1)] = load_w1(1, 1)
        w1_raw[(2, 1)] = load_w1(2, 1)
        w5_raw = [load_w5(0)]
        view1 = placed([P, PACK, M], F32, "view1", VIEW1_AT)
        nc.sync.dma_start(out=view1[:], in_=rows4(view, PASS, 0, M))
        w5_raw.append(load_w5(1))
        shift_sb = placed([P, PACK, M], F32, "shift_sb", SHIFT_AT)
        nc.sync.dma_start(out=shift_sb[:], in_=rows4(shift, 0, 0, M))
        w4_codes = keep.tile([P, 2, 2 * N], U8, name="w4_codes", align_bytes=64)
        nc.sync.dma_start(
            out=w4_codes[:].bitcast(I32), in_=w4_words.rearrange("b p c -> p b c").bitcast(I32)
        )
        for quad in range(QUADRANTS):
            nc.sync.dma_start(
                out=w4_scale[32 * quad : 32 * quad + 4, :, :].bitcast(I32),
                in_=w4_scales[:, 4 * quad : 4 * quad + 4, :].rearrange("b r c -> r b c").bitcast(I32),
            )
        wgo_sb = keep.tile([P, M], F32, name="wgo_sb")
        nc.sync.dma_start(out=wgo_sb[:], in_=wgo)
        nc.sync.dma_start(idx3[:], offs3)

        rounded = rounded_tile("w1r20")
        deal_round(nc.scalar.copy, rounded[:], last_raw[0], 0)
        deal_round(nc.vector.tensor_copy, rounded[:], last_raw[1], side_width // PACK)
        w1_mx = w1_tiles(K_PASSES - 1, 0)
        for i in range(PACK):
            cols = slice(P * i, P * (i + 1))
            quantise(w1_mx[0][:, cols], w1_mx[1][:, cols], rounded[:, PASS * i : PASS * (i + 1)])
            h_pass(banks0, w1_mx, K_PASSES - 1, i, False, True)

        z0_bytes = keep.tile([P, (PACK + 1) * M], F32, name="z0", align_bytes=64)
        z0 = z0_bytes[:, 0 : PACK * M].rearrange("p (i m) -> p i m", i=PACK)

        def prepare0(i):
            h = empty_h(banks0, 0, i)
            pair = view0[i // 2]
            if i % 2 == 0:
                nc.vector.tensor_tensor(
                    out=pair[:], in0=pair[:], in1=wgt_sb[:].unsqueeze(1).to_broadcast([P, 2, M]), op=MULT
                )
            return h, pair[:, i % 2, :]

        def gather0(i, h, factor):
            nc.vector.tensor_tensor(out=z0[:, i, :], in0=h[:].indirect(idx2[:]), in1=factor, op=MULT)

        banks1 = h_banks(1)
        gather0(0, *prepare0(0))
        gather0(1, *prepare0(1))
        w1_mx0 = w1_operand(0, 1, nc.scalar.copy, rounded_tile("w1r01")[:])
        gather0(2, *prepare0(2))
        last_plane = prepare0(3)
        for i in range(PACK):
            h_pass(banks1, w1_mx0, 0, i, True, False)
        w1_mx2 = w1_operand(2, 1, nc.vector.tensor_copy, rounded_tile("w1r21")[:])
        w1_mx1 = w1_operand(1, 1, nc.scalar.copy, z0_bytes[:, (PACK - 1) * M : (PACK + 1) * M].bitcast(BF16))
        gather0(3, *last_plane)

        w5_mx = []

        def w5_operand(b, rounded):
            deal_round(nc.scalar.copy, rounded, w5_raw[b], 0)
            codes = keep.tile([P, N], U32, name="w5c%d" % b, align_bytes=64)
            scales = keep.tile([P, N], U8, name="w5s%d" % b, align_bytes=64)
            quantise(codes[:], scales[:], rounded)
            w5_mx.append((codes, scales))

        h1 = []
        for i in range(PACK):
            h_pass(banks1, w1_mx2, 2, i, False, False)
            h_pass(banks1, w1_mx1, 1, i, False, True)
            h1.append(empty_h(banks1, 1, i))
        w5_operand(0, rounded_tile("w5r0")[:])

        x1_bytes = placed([P, PACK * SLOT], F32, "x1", X1_AT)
        x1 = (
            x1_bytes[:, SLOT : 2 * SLOT].rearrange("p (i m) -> p i m", i=PACK),
            x1_bytes[:].rearrange("p (i m) -> p i m", i=PACK)[:, :, 0:HALF],
        )

        def list_half(entries, u):
            return entries[:, HALF // GROUP * u : HALF // GROUP * (u + 1)]

        def gather1(u, i):
            nc.vector.tensor_tensor(
                out=x1[u][:, i, :],
                in0=h1[i][:].indirect(list_half(idx2, u)),
                in1=view1[:, i, HALF * u : HALF * (u + 1)],
                op=MULT,
            )

        def round_z0(u):
            rounded = placed([P, PACK * HALF], BF16, "z0r%d" % u, Z0_AT[u])
            nc.scalar.copy(
                out=rounded[:].rearrange("p (s e i) -> p s i e", e=4, i=PACK),
                in_=z0[:, :, HALF * u : HALF * (u + 1)].rearrange("p i (s e) -> p s i e", e=4),
            )
            return rounded

        def round_z1(u):
            rounded = placed([P, PACK * HALF], BF16, "z1r%d" % u, Z1_AT[u])
            weight = wgt_sb[:, HALF * u : HALF * (u + 1)].rearrange("p (s e) -> p s e", e=2)
            nc.vector.tensor_tensor(
                out=rounded[:].rearrange("p (s e i) -> p s i e", e=2, i=PACK),
                in0=x1[u].rearrange("p i (s e) -> p s i e", e=2),
                in1=weight.unsqueeze(2).to_broadcast([P, HALF // 2, PACK, 2]),
                op=MULT,
            )
            return rounded

        def z_operand(b, u, rounded):
            codes = keep.tile([P, HALF], U32, name="z%d%d_codes" % (b, u), align_bytes=64)
            scales = keep.tile([P, HALF], U8, name="z%d%d_scale" % (b, u), align_bytes=64)
            quantise(codes[:], scales[:], rounded[:])
            return codes, scales

        def sums_pass(sums, z_mx, b):
            codes, scales = z_mx
            for w, (e4, e5) in enumerate(sums):
                cols = slice(P * w, P * (w + 1))
                nc.tensor.matmul_mx(
                    out=e4[:], lhsT=codes[:, cols].bitcast(FP8X4), lhsT_scale=scales[:, cols],
                    rhs=w4_codes[:, b, :].bitcast(FP4X4), rhs_scale=w4_scale[:, b, :],
                    start=(b == 0), stop=(b == 1),
                )
                nc.tensor.matmul_mx(
                    out=e5[:], lhsT=codes[:, cols].bitcast(FP8X4), lhsT_scale=scales[:, cols],
                    rhs=w5_mx[b][0][:].bitcast(FP8X4), rhs_scale=w5_mx[b][1][:],
                    start=(b == 0), stop=(b == 1),
                )

        def open_sums(u):
            z_mx = z_operand(0, u, round_z0(u))
            sums = [(bank("e4_%d" % c), bank("e5_%d" % c)) for c in (2 * u, 2 * u + 1)]
            sums_pass(sums, z_mx, 0)
            return sums

        def larger_of(c, e4, e5, e4_sb):
            nc.scalar.copy(
                out=e4_sb.rearrange("m (i p) -> m i p", i=PACK),
                in_=e4[:].rearrange("m (p i) -> m i p", i=PACK),
            )
            larger = ring.tile([P, N], F32, name="larger%d" % c, tag="larger", bufs=M // P)
            nc.vector.tensor_tensor(out=larger[:], in0=e5[:], in1=e4_sb, op=MAX)
            return larger

        def e4_tile(c):
            return placed([P, N], F32, "e4_sb%d" % c, E4_AT[c])[:]

        def y_bank(c, larger):
            turned = bank("shift_ps%d" % c)
            for i in range(PACK):
                nc.tensor.transpose(turned[:, P * i : P * (i + 1)], shift_sb[:, i, P * c : P * (c + 1)], ident[:])
            shift_t = ring.tile([P, BANK], F32, name="shift_t%d" % c, tag="shift_t", bufs=2)
            nc.scalar.copy(out=shift_t[:], in_=turned[:])
            y_ps = bank("y_ps%d" % c)
            for i in range(PACK):
                cols = slice(P * i, P * (i + 1))
                nc.tensor.matmul(
                    y_ps[:, cols], shift_t[:, cols], ident[:], start=(i == 0), stop=False, is_transpose=True
                )
            for i in range(PACK):
                cols = slice(P * i, P * (i + 1))
                nc.tensor.matmul(
                    y_ps[:, cols], larger[:, cols], ident[:], start=False, stop=(i == PACK - 1), is_transpose=True
                )
            return y_ps

        def empty_y(y_ps, y, w, i0):
            nc.scalar.copy(
                out=y[:, :, P * w : P * (w + 1)],
                in_=y_ps[:].rearrange("p (i m) -> p i m", i=PACK)[:, i0 : i0 + y.shape[1], :],
            )

        def place(u, i, y_plane):
            nc.vector.tensor_tensor(
                out=pages[i][:].indirect(list_half(idx3, u)),
                in0=y_plane,
                in1=wgo_sb[:, HALF * u : HALF * (u + 1)],
                op=MULT,
            )

        gather1(0, 0)
        gather1(1, 0)
        for i in range(1, PACK):
            gather1(0, i)
        sums = open_sums(0)
        rounded = round_z1(0)
        gather1(1, 1)
        z_mx = z_operand(1, 0, rounded)
        w5_operand(1, x1_bytes[:, 2 * SLOT : 3 * SLOT].bitcast(BF16))
        sums_pass(sums, z_mx, 1)
        gather1(1, 2)
        e4_first = (e4_tile(0), x1_bytes[:, 3 * SLOT : 3 * SLOT + N])
        larger = [larger_of(c, *sums[c], e4_first[c]) for c in range(2)]
        gather1(1, 3)
        y_first = []
        y_early = placed([P, EARLY_PLANES, HALF], F32, "y_early", Y_EARLY_AT)
        for c in range(2):
            y_first.append(y_bank(c, larger[c]))
            empty_y(y_first[c], y_early, c, 0)

        sums = open_sums(1)
        sums_pass(sums, z_operand(1, 1, round_z1(1)), 1)
        larger = [larger_of(2 + w, *sums[w], e4_tile(2 + w)) for w in range(2)]
        for i in range(EARLY_PLANES):
            place(0, i, y_early[:, i, :])
        y_late = placed([P, PACK - EARLY_PLANES, HALF], F32, "y_late", Y_LATE_AT)
        for c in range(2):
            empty_y(y_first[c], y_late, c, EARLY_PLANES)
        y_second = placed([P, PACK, HALF], F32, "y_second", Y_SECOND_AT)
        for w in range(2):
            empty_y(y_bank(2 + w, larger[w]), y_second, w, 0)
        for i in range(EARLY_PLANES, PACK):
            place(0, i, y_late[:, i - EARLY_PLANES, :])
        for i in range(PACK):
            place(1, i, y_second[:, i, :])
            nc.sync.dma_start(out=rows4(out, 0, 0, T2)[:, i, :], in_=pages[i][:])
